import numpy as np
import ml_dtypes


def mxq(x, axis, fmt="e4m3"):
    dtype, down = {"e4m3": (ml_dtypes.float8_e4m3fn, 7), "e5m2": (ml_dtypes.float8_e5m2, 14)}[fmt]
    v = np.moveaxis(np.asarray(x, np.float32).astype(ml_dtypes.bfloat16).astype(np.float64), axis, -1)
    blocks = v.reshape(v.shape[:-1] + (-1, 32))
    amax = np.abs(blocks).max(-1, keepdims=True)
    byte = np.maximum(np.where(amax > 0, np.frexp(amax)[1] - 1 + 127, 0) - down, 1)
    scale = np.exp2(byte - 127.0)
    codes = (blocks / scale).astype(np.float32).astype(dtype).astype(np.float64)
    return np.moveaxis((codes * scale).reshape(v.shape), -1, axis)


WIDE = False


def mx_kscale(k, group=512):
    if not WIDE:
        return np.ones(k)
    levels = np.array([18, -18])
    if group != 512:
        return np.exp2(np.random.permutation(np.resize(levels, k // group))).repeat(group)
    if k % 512:
        return np.exp2(np.random.permutation(np.resize(levels, k // 32))).repeat(32)
    a = np.empty((k // 512, 16))
    for p in range(k // 512):
        a[p, :8] = np.random.permutation(np.resize(levels, 8))
        for g in range(8):
            far = levels[np.abs(levels - a[p, g]) >= 10]
            a[p, g + 8] = far[np.random.randint(len(far))]
    return np.exp2(a.ravel()).repeat(32)


def f64(x):
    return np.asarray(x).astype(np.float64)


G, D, K, M, N = 4, 128, 1024, 128, 512


def setup_inputs():
    n = np.random.standard_normal
    s = mx_kscale(D, 0)[:, None]
    u = mx_kscale(K)[:, None]
    return {
        "x": (n((G, D, N)) * s).astype(np.float32),
        "w1": (n((G, D, K)) / np.sqrt(D) / s).astype(np.float32),
        "hs": (np.random.uniform(0.5, 2.0, (G, K, 1)) * u).astype(np.float32),
        "w2": (n((G, K, M)) / np.sqrt(K) / u).astype(np.float32),
        "b": (0.5 * n((G, K, 1))).astype(np.float32),
    }


def reference(x, w1, hs, w2, b):
    xq = mxq(f64(x), 1, "e4m3")
    h = mxq(f64(w1), 1, "e4m3").transpose(0, 2, 1) @ xq
    h = h + f64(b)
    h = (np.square(np.maximum(h, 0.0))) * f64(hs)
    y = mxq(f64(w2), 1, "e4m3").transpose(0, 2, 1) @ mxq(h, 1, "e4m3")
    return y

@@ -1,0 +1,284 @@
+from contextlib import ExitStack
+
+import concourse.mybir as mybir
+
+G, D, K, M, N = 4, 128, 1024, 128, 512
+FLOPS = 2 * G * N * (D * K + K * M)
+
+F32 = mybir.dt.float32
+BF16 = mybir.dt.bfloat16
+U32 = mybir.dt.uint32
+U8 = mybir.dt.uint8
+FP8X4 = mybir.dt.float8_e4m3fn_x4
+ALU = mybir.AluOpType
+ACT = mybir.ActivationFunctionType
+
+P = 128
+PACK = 4
+ROWS = D // PACK
+K_PASS = P * PACK
+PASSES = K // K_PASS
+UNITS = G * PASSES
+RUN = 2
+QUAD = 32
+TINY = 2.0 ** -100
+SCALAR_COLS = 144
+SCALAR_COLS_LAST = 256
+SCALAR_COLS_6 = 288
+AHEAD = 2
+G1_SCALAR = True
+W1_SCALAR = 48
+X_SCALAR = 96
+
+
+def tile_rows_gmlp_relu2_bias_kernel(tc, x, w1, hs, w2, b, out):
+    nc = tc.nc
+
+    def runs_of_rows(rows):
+        return rows.rearrange("p j (c i) -> p c j i", i=RUN)
+
+    def runs_of_words(words):
+        return words.rearrange("p (c i) j -> p c j i", i=RUN)
+
+    def quantize(codes, scales, words):
+        nc.vector.quantize_mx(out=codes.bitcast(FP8X4), scales=scales, in_=words.rearrange("p c j -> p (c j)"))
+
+    with ExitStack() as ctx:
+        sb = ctx.enter_context(tc.tile_pool(name="sb", bufs=1))
+        ps = ctx.enter_context(tc.psum_pool(name="ps", bufs=1))
+        ctx.enter_context(tc.manual_schedule())
+
+        def sbuf(name, shape, dtype):
+            return sb.tile(shape, dtype, name=name, align_bytes=64)
+
+        def vector_copy(o, i):
+            nc.vector.tensor_copy(out=o, in_=i)
+
+        def scalar_copy(o, i):
+            nc.scalar.copy(out=o, in_=i)
+
+        vec_raw = sbuf("vec_raw", [P, P], F32)
+        nc.vector.memset(vec_raw[:], 0.0)
+        for place, vec in enumerate((b, hs)):
+            nc.scalar.dma_start(
+                out=vec_raw[place:P:PACK, :],
+                in_=vec.rearrange("g (q d w) o -> d (g q) (w o)", q=PASSES, d=P // QUAD),
+            )
+
+        x_rows = x.rearrange("g (p j) n -> (g p) j n", j=PACK)
+        w1_rows = w1.rearrange("g (p j) k -> (g p) j k", j=PACK)
+        w1_raw = [sbuf("w1_raw%d" % q, [P, PACK, K_PASS], F32) for q in range(PASSES)]
+        x_raw = [sbuf("x_raw%d" % h, [P, PACK, N // 2], F32) for h in range(2)]
+        w2_raw = [sbuf("w2_raw%d" % g, [P, PASSES, PACK, M], F32) for g in range(G)]
+
+        def load_w1(q):
+            nc.sync.dma_start(out=w1_raw[q][:], in_=w1_rows[:, :, q * K_PASS : (q + 1) * K_PASS])
+
+        def load_w2(g):
+            nc.sync.dma_start(
+                out=w2_raw[g][:].rearrange("p q j m -> p q (j m)"),
+                in_=w2[g].rearrange("(q p j) m -> p q (j m)", q=PASSES, j=PACK),
+            )
+
+        load_w1(0)
+        for h in range(2):
+            nc.sync.dma_start(out=x_raw[h][:], in_=x_rows[:, :, h * (N // 2) : (h + 1) * (N // 2)])
+        load_w2(0)
+        load_w2(1)
+        load_w1(1)
+        load_w2(2)
+        load_w2(3)
+
+        vec_dealt = sbuf("vec_dealt", [P, PACK, QUAD], F32)
+        vec_t = sbuf("vec_t", [P, PACK, QUAD], F32)
+        nc.vector.tensor_copy(out=vec_dealt[:], in_=vec_raw[:].rearrange("p (a r) -> p r a", r=PACK))
+        nc.vector.transpose(out=vec_t[:].rearrange("p r c -> p (r c)"), in_=vec_dealt[:].rearrange("p r a -> p (r a)"))
+        vec_cols = vec_t[:].rearrange("p r (u w) -> p u r w", w=PACK)
+        b_tab = vec_cols[:, :, :, 0]
+        hs_tab = vec_cols[:, :, :, 1]
+        mag = sbuf("mag", [P, UNITS, PACK], F32)
+        root0 = sbuf("root0", [P, UNITS, PACK], F32)
+        sgn = sbuf("sgn", [P, UNITS, PACK], F32)
+        inv = sbuf("inv", [P, UNITS, PACK], F32)
+        half_q = sbuf("half_q", [P, UNITS, PACK], F32)
+        root = sbuf("root", [P, UNITS, PACK], F32)
+        root_b = sbuf("root_b", [P, UNITS, PACK], F32)
+        nc.vector.scalar_tensor_tensor(out=mag[:], in0=hs_tab, scalar=-1.0, in1=hs_tab, op0=ALU.mult, op1=ALU.max)
+        nc.scalar.activation(out=root0[:], in_=mag[:], func=ACT.Sqrt, bias=TINY)
+        nc.scalar.activation(out=sgn[:], in_=hs_tab, func=ACT.Sign)
+
+        w1_bf = [sbuf("w1_bf%d" % q, [P, K_PASS, PACK], BF16) for q in range(PASSES)]
+        w1_codes = [sbuf("w1_codes%d" % q, [P, K_PASS], U32) for q in range(PASSES)]
+        w1_scales = [sbuf("w1_scales%d" % q, [P, K_PASS], U8) for q in range(PASSES)]
+        x_bf = [sbuf("x_bf%d" % h, [P, N // 2, PACK], BF16) for h in range(2)]
+        x_codes = sbuf("x_codes", [P, N], U32)
+        x_scales = sbuf("x_scales", [P, N], U8)
+
+        def round_w1(q, copy, ms):
+            copy(
+                w1_bf[q][:].rearrange("p (r m) j -> p m j r", r=PACK)[:, ms, :, :],
+                w1_raw[q][:].rearrange("p j (m r) -> p m j r", r=PACK)[:, ms, :, :],
+            )
+
+        def round_x(h, copy, cols):
+            copy(runs_of_words(x_bf[h][:, cols, :]), runs_of_rows(x_raw[h][:, :, cols]))
+
+        def quantize_w1(q):
+            quantize(w1_codes[q][:], w1_scales[q][:], w1_bf[q][:])
+
+        def quantize_x(h):
+            cols = slice(h * (N // 2), (h + 1) * (N // 2))
+            quantize(x_codes[:, cols], x_scales[:, cols], x_bf[h][:])
+
+        nc.vector.reciprocal(out=inv[:], in_=root0[:])
+        nc.vector.scalar_tensor_tensor(out=half_q[:], in0=mag[:], scalar=0.5, in1=inv[:], op0=ALU.mult, op1=ALU.mult)
+        round_w1(0, vector_copy, slice(0, P))
+        nc.vector.scalar_tensor_tensor(out=root[:], in0=root0[:], scalar=0.5, in1=half_q[:], op0=ALU.mult, op1=ALU.add)
+        quantize_w1(0)
+        nc.vector.tensor_tensor(out=root_b[:], in0=root[:], in1=b_tab, op=ALU.mult)
+        round_x(0, scalar_copy, slice(0, N // 2))
+        round_x(1, scalar_copy, slice(0, X_SCALAR))
+        round_x(1, vector_copy, slice(X_SCALAR, N // 2))
+        quantize_x(0)
+        quantize_x(1)
+
+        w2_bf = [sbuf("w2_bf%d" % c, [P, M, PACK], BF16) for c in range(UNITS)]
+        w2_codes = [sbuf("w2_codes%d" % c, [P, M], U32) for c in range(UNITS)]
+        w2_scales = [sbuf("w2_scales%d" % c, [P, M], U8) for c in range(UNITS)]
+
+        def round_w2(g, q):
+            c = g * PASSES + q
+            nc.vector.tensor_tensor(
+                out=runs_of_words(w2_bf[c][:]),
+                in0=runs_of_rows(w2_raw[g][:, q, :, :]),
+                in1=sgn[:, c, :].unsqueeze(1).unsqueeze(3).to_broadcast([P, M // RUN, PACK, RUN]),
+                op=ALU.mult,
+            )
+
+        def quantize_w2(g, q):
+            c = g * PASSES + q
+            quantize(w2_codes[c][:], w2_scales[c][:], w2_bf[c][:])
+
+        early = [(g, q) for g in range(2) for q in range(PASSES)]
+        late = [(g, q) for g in range(2, G) for q in range(PASSES)]
+        round_w2(*early[0])
+        for i in range(1, len(early)):
+            round_w2(*early[i])
+            quantize_w2(*early[i - 1])
+        round_w1(1, vector_copy, slice(0, P))
+        quantize_w2(*early[-1])
+        quantize_w1(1)
+
+        n_banks = [2, 1, 1, 2]
+        banks = [[ps.tile([P, N], F32, name="z%d_%d" % (g, i)) for i in range(n_banks[g])] for g in range(G)]
+        acc = [ps.tile([P, N], F32, name="acc%d" % i) for i in range(2)]
+        act = [sbuf("act%d" % u, [P, PACK, N], F32) for u in range(UNITS)]
+        h_bf = [sbuf("h_bf%d" % u, [P, N, PACK], BF16) for u in range(UNITS)]
+        h_codes = [sbuf("h_codes%d" % u, [P, N], U32) for u in range(UNITS)]
+        h_scales = [sbuf("h_scales%d" % u, [P, N], U8) for u in range(UNITS)]
+        res = [sbuf("res%d" % g, [P, N], F32) for g in range(G)]
+
+        steps = sorted(((u, r) for u in range(UNITS) for r in range(PACK)), key=lambda s: 4 * s[0] + 3 * s[1])
+
+        def bank_of(u, r):
+            g, q = u % G, u // G
+            return banks[g][(q * PACK + r) % n_banks[g]]
+
+        def first_layer(u, r):
+            g, q = u % G, u // G
+            rows = slice(g * ROWS, (g + 1) * ROWS)
+            cols = slice(r * P, (r + 1) * P)
+            nc.tensor.matmul_mx(
+                out=bank_of(u, r)[:],
+                lhsT=w1_codes[q][rows, cols].bitcast(FP8X4),
+                lhsT_scale=w1_scales[q][rows, cols],
+                rhs=x_codes[rows, :].bitcast(FP8X4),
+                rhs_scale=x_scales[rows, :],
+                start=True,
+                stop=True,
+            )
+
+        def relu(u, r):
+            g, q = u % G, u // G
+            c = g * PASSES + q
+            nc.scalar.activation(
+                out=act[u][:, r, :],
+                in_=bank_of(u, r)[:],
+                func=ACT.Relu,
+                scale=root[:, c, r : r + 1],
+                bias=root_b[:, c, r : r + 1],
+            )
+
+        def scalar_cols(u):
+            return SCALAR_COLS_LAST if u == UNITS - 1 else (SCALAR_COLS_6 if u == UNITS - 2 else SCALAR_COLS)
+
+        def square_vector(u):
+            rows = runs_of_rows(act[u][:, :, scalar_cols(u) :])
+            nc.vector.tensor_tensor(out=runs_of_words(h_bf[u][:, scalar_cols(u) :, :]), in0=rows, in1=rows, op=ALU.mult)
+
+        def square_scalar(u):
+            nc.scalar.activation(
+                out=runs_of_words(h_bf[u][:, : scalar_cols(u), :]),
+                in_=runs_of_rows(act[u][:, :, : scalar_cols(u)]),
+                func=ACT.Square,
+            )
+
+        def second_layer(g, q):
+            u, c = q * G + g, g * PASSES + q
+            nc.tensor.matmul_mx(
+                out=acc[g % 2][:],
+                lhsT=w2_codes[c][:].bitcast(FP8X4),
+                lhsT_scale=w2_scales[c][:],
+                rhs=h_codes[u][:].bitcast(FP8X4),
+                rhs_scale=h_scales[u][:],
+                start=(q == 0),
+                stop=(q == PASSES - 1),
+            )
+
+        def store(g, engine_copy):
+            engine_copy(res[g][:], acc[g % 2][:])
+            nc.sync.dma_start(out=out[g], in_=res[g][:])
+
+        def quantize_h(u, cols):
+            quantize(h_codes[u][:, cols], h_scales[u][:, cols], h_bf[u][:, cols, :])
+
+        def finish(u):
+            square_scalar(u)
+            if u < len(late):
+                round_w2(*late[u])
+            if u == G + 1:
+                store(0, vector_copy)
+            if u == G + 2 and not G1_SCALAR:
+                store(1, vector_copy)
+            quantize_h(u, slice(0, N))
+            if u < len(late):
+                quantize_w2(*late[u])
+
+        for s in steps[:AHEAD]:
+            first_layer(*s)
+        pending = None
+        for i, (u, r) in enumerate(steps):
+            relu(u, r)
+            if i + AHEAD < len(steps):
+                first_layer(*steps[i + AHEAD])
+            if pending is not None:
+                finish(pending)
+                pending = None
+            if r == PACK - 1:
+                square_vector(u)
+                pending = u
+                if u - 1 in (0, 1, G, G + 1):
+                    second_layer((u - 1) % G, (u - 1) // G)
+                if u == G + 2:
+                    second_layer(2, 0)
+        last = UNITS - 1
+        second_layer(2, 1)
+        if G1_SCALAR:
+            store(1, scalar_copy)
+        second_layer(3, 0)
+        square_scalar(last)
+        quantize_h(last, slice(N // 2, N))
+        quantize_h(last, slice(0, N // 2))
+        second_layer(G - 1, 1)
+        store(G - 2, scalar_copy)
+        store(G - 1, vector_copy)

@@ -22,13 +22,11 @@ UNITS = G * PASSES
 RUN = 2
 QUAD = 32
 TINY = 2.0 ** -100
-SCALAR_COLS = 144
+SCALAR_COLS = 160
 SCALAR_COLS_LAST = 256
-SCALAR_COLS_6 = 288
+SCALAR_COLS_6 = 256
 AHEAD = 2
 G1_SCALAR = True
-W1_SCALAR = 48
-X_SCALAR = 96
 
 
 def tile_rows_gmlp_relu2_bias_kernel(tc, x, w1, hs, w2, b, out):
@@ -59,16 +57,10 @@ def tile_rows_gmlp_relu2_bias_kernel(tc, x, w1, hs, w2, b, out):
 
         vec_raw = sbuf("vec_raw", [P, P], F32)
         nc.vector.memset(vec_raw[:], 0.0)
-        for place, vec in enumerate((b, hs)):
-            nc.scalar.dma_start(
-                out=vec_raw[place:P:PACK, :],
-                in_=vec.rearrange("g (q d w) o -> d (g q) (w o)", q=PASSES, d=P // QUAD),
-            )
 
-        x_rows = x.rearrange("g (p j) n -> (g p) j n", j=PACK)
+        x_raw = sbuf("x_raw", [P, PACK, N], F32)
         w1_rows = w1.rearrange("g (p j) k -> (g p) j k", j=PACK)
         w1_raw = [sbuf("w1_raw%d" % q, [P, PACK, K_PASS], F32) for q in range(PASSES)]
-        x_raw = [sbuf("x_raw%d" % h, [P, PACK, N // 2], F32) for h in range(2)]
         w2_raw = [sbuf("w2_raw%d" % g, [P, PASSES, PACK, M], F32) for g in range(G)]
 
         def load_w1(q):
@@ -80,18 +72,28 @@ def tile_rows_gmlp_relu2_bias_kernel(tc, x, w1, hs, w2, b, out):
                 in_=w2[g].rearrange("(q p j) m -> p q (j m)", q=PASSES, j=PACK),
             )
 
+        nc.sync.dma_start(
+            out=x_raw[:].rearrange("p j n -> p (j n)"), in_=x.rearrange("g (p j) n -> (g p) (j n)", j=PACK)
+        )
+        for place, vec in enumerate((b, hs)):
+            nc.sync.dma_start(
+                out=vec_raw[place:P:PACK, :],
+                in_=vec.rearrange("g (q d w) o -> d (g q) (w o)", q=PASSES, d=P // QUAD),
+            )
         load_w1(0)
-        for h in range(2):
-            nc.sync.dma_start(out=x_raw[h][:], in_=x_rows[:, :, h * (N // 2) : (h + 1) * (N // 2)])
-        load_w2(0)
-        load_w2(1)
+        for g in range(G - 1):
+            load_w2(g)
         load_w1(1)
-        load_w2(2)
-        load_w2(3)
+        load_w2(G - 1)
+
+        x_bf = sbuf("x_bf", [P, N, PACK], BF16)
+        x_codes = sbuf("x_codes", [P, N], U32)
+        x_scales = sbuf("x_scales", [P, N], U8)
 
         vec_dealt = sbuf("vec_dealt", [P, PACK, QUAD], F32)
         vec_t = sbuf("vec_t", [P, PACK, QUAD], F32)
         nc.vector.tensor_copy(out=vec_dealt[:], in_=vec_raw[:].rearrange("p (a r) -> p r a", r=PACK))
+        vector_copy(runs_of_words(x_bf[:]), runs_of_rows(x_raw[:]))
         nc.vector.transpose(out=vec_t[:].rearrange("p r c -> p (r c)"), in_=vec_dealt[:].rearrange("p r a -> p (r a)"))
         vec_cols = vec_t[:].rearrange("p r (u w) -> p u r w", w=PACK)
         b_tab = vec_cols[:, :, :, 0]
@@ -107,40 +109,29 @@ def tile_rows_gmlp_relu2_bias_kernel(tc, x, w1, hs, w2, b, out):
         nc.scalar.activation(out=root0[:], in_=mag[:], func=ACT.Sqrt, bias=TINY)
         nc.scalar.activation(out=sgn[:], in_=hs_tab, func=ACT.Sign)
 
-        w1_bf = [sbuf("w1_bf%d" % q, [P, K_PASS, PACK], BF16) for q in range(PASSES)]
-        w1_codes = [sbuf("w1_codes%d" % q, [P, K_PASS], U32) for q in range(PASSES)]
-        w1_scales = [sbuf("w1_scales%d" % q, [P, K_PASS], U8) for q in range(PASSES)]
-        x_bf = [sbuf("x_bf%d" % h, [P, N // 2, PACK], BF16) for h in range(2)]
-        x_codes = sbuf("x_codes", [P, N], U32)
-        x_scales = sbuf("x_scales", [P, N], U8)
+        halves = [(q, h) for q in range(PASSES) for h in range(PACK // RUN)]
+        w1_bf = {k: sbuf("w1_bf%d%d" % k, [P, RUN * P, PACK], BF16) for k in halves}
+        w1_codes = {k: sbuf("w1_codes%d%d" % k, [P, RUN * P], U32) for k in halves}
+        w1_scales = {k: sbuf("w1_scales%d%d" % k, [P, RUN * P], U8) for k in halves}
 
-        def round_w1(q, copy, ms):
+        def round_w1(q, h, copy):
             copy(
-                w1_bf[q][:].rearrange("p (r m) j -> p m j r", r=PACK)[:, ms, :, :],
-                w1_raw[q][:].rearrange("p j (m r) -> p m j r", r=PACK)[:, ms, :, :],
+                w1_bf[q, h][:].rearrange("p (r m) j -> p m j r", r=RUN),
+                w1_raw[q][:].rearrange("p j (m r) -> p m j r", r=PACK)[:, :, :, h * RUN : (h + 1) * RUN],
             )
 
-        def round_x(h, copy, cols):
-            copy(runs_of_words(x_bf[h][:, cols, :]), runs_of_rows(x_raw[h][:, :, cols]))
+        def quantize_w1(q, h):
+            quantize(w1_codes[q, h][:], w1_scales[q, h][:], w1_bf[q, h][:])
 
-        def quantize_w1(q):
-            quantize(w1_codes[q][:], w1_scales[q][:], w1_bf[q][:])
-
-        def quantize_x(h):
-            cols = slice(h * (N // 2), (h + 1) * (N // 2))
-            quantize(x_codes[:, cols], x_scales[:, cols], x_bf[h][:])
-
+        quantize(x_codes[:], x_scales[:], x_bf[:])
+        round_w1(0, 0, vector_copy)
+        round_w1(0, 1, scalar_copy)
         nc.vector.reciprocal(out=inv[:], in_=root0[:])
+        quantize_w1(0, 0)
         nc.vector.scalar_tensor_tensor(out=half_q[:], in0=mag[:], scalar=0.5, in1=inv[:], op0=ALU.mult, op1=ALU.mult)
-        round_w1(0, vector_copy, slice(0, P))
+        quantize_w1(0, 1)
         nc.vector.scalar_tensor_tensor(out=root[:], in0=root0[:], scalar=0.5, in1=half_q[:], op0=ALU.mult, op1=ALU.add)
-        quantize_w1(0)
         nc.vector.tensor_tensor(out=root_b[:], in0=root[:], in1=b_tab, op=ALU.mult)
-        round_x(0, scalar_copy, slice(0, N // 2))
-        round_x(1, scalar_copy, slice(0, X_SCALAR))
-        round_x(1, vector_copy, slice(X_SCALAR, N // 2))
-        quantize_x(0)
-        quantize_x(1)
 
         w2_bf = [sbuf("w2_bf%d" % c, [P, M, PACK], BF16) for c in range(UNITS)]
         w2_codes = [sbuf("w2_codes%d" % c, [P, M], U32) for c in range(UNITS)]
@@ -159,15 +150,11 @@ def tile_rows_gmlp_relu2_bias_kernel(tc, x, w1, hs, w2, b, out):
             c = g * PASSES + q
             quantize(w2_codes[c][:], w2_scales[c][:], w2_bf[c][:])
 
-        early = [(g, q) for g in range(2) for q in range(PASSES)]
-        late = [(g, q) for g in range(2, G) for q in range(PASSES)]
+        early = [(g, q) for g in range(G - 1) for q in range(PASSES)]
         round_w2(*early[0])
         for i in range(1, len(early)):
             round_w2(*early[i])
             quantize_w2(*early[i - 1])
-        round_w1(1, vector_copy, slice(0, P))
-        quantize_w2(*early[-1])
-        quantize_w1(1)
 
         n_banks = [2, 1, 1, 2]
         banks = [[ps.tile([P, N], F32, name="z%d_%d" % (g, i)) for i in range(n_banks[g])] for g in range(G)]
@@ -180,6 +167,8 @@ def tile_rows_gmlp_relu2_bias_kernel(tc, x, w1, hs, w2, b, out):
 
         steps = sorted(((u, r) for u in range(UNITS) for r in range(PACK)), key=lambda s: 4 * s[0] + 3 * s[1])
 
+        steps[1:3] = [steps[2], steps[1]]
+
         def bank_of(u, r):
             g, q = u % G, u // G
             return banks[g][(q * PACK + r) % n_banks[g]]
@@ -187,11 +176,11 @@ def tile_rows_gmlp_relu2_bias_kernel(tc, x, w1, hs, w2, b, out):
         def first_layer(u, r):
             g, q = u % G, u // G
             rows = slice(g * ROWS, (g + 1) * ROWS)
-            cols = slice(r * P, (r + 1) * P)
+            cols = slice(r % RUN * P, (r % RUN + 1) * P)
             nc.tensor.matmul_mx(
                 out=bank_of(u, r)[:],
-                lhsT=w1_codes[q][rows, cols].bitcast(FP8X4),
-                lhsT_scale=w1_scales[q][rows, cols],
+                lhsT=w1_codes[q, r // RUN][rows, cols].bitcast(FP8X4),
+                lhsT_scale=w1_scales[q, r // RUN][rows, cols],
                 rhs=x_codes[rows, :].bitcast(FP8X4),
                 rhs_scale=x_scales[rows, :],
                 start=True,
@@ -235,24 +224,30 @@ def tile_rows_gmlp_relu2_bias_kernel(tc, x, w1, hs, w2, b, out):
                 stop=(q == PASSES - 1),
             )
 
-        def store(g, engine_copy):
-            engine_copy(res[g][:], acc[g % 2][:])
-            nc.sync.dma_start(out=out[g], in_=res[g][:])
+        def store(g, engine_copy, cols=slice(0, N)):
+            engine_copy(res[g][:, cols], acc[g % 2][:, cols])
+            nc.sync.dma_start(out=out[g][:, cols], in_=res[g][:, cols])
 
         def quantize_h(u, cols):
             quantize(h_codes[u][:, cols], h_scales[u][:, cols], h_bf[u][:, cols, :])
 
         def finish(u):
             square_scalar(u)
-            if u < len(late):
-                round_w2(*late[u])
+            if u == 0:
+                quantize_w2(*early[-1])
+            if u < 2:
+                round_w1(1, u, vector_copy)
+            elif u < 4:
+                round_w2(G - 1, u - 2)
             if u == G + 1:
                 store(0, vector_copy)
             if u == G + 2 and not G1_SCALAR:
                 store(1, vector_copy)
             quantize_h(u, slice(0, N))
-            if u < len(late):
-                quantize_w2(*late[u])
+            if u < 2:
+                quantize_w1(1, u)
+            elif u < 4:
+                quantize_w2(G - 1, u - 2)
 
         for s in steps[:AHEAD]:
             first_layer(*s)
@@ -281,4 +276,5 @@ def tile_rows_gmlp_relu2_bias_kernel(tc, x, w1, hs, w2, b, out):
         quantize_h(last, slice(0, N // 2))
         second_layer(G - 1, 1)
         store(G - 2, scalar_copy)
-        store(G - 1, vector_copy)
+        store(G - 1, vector_copy, slice(0, N // 2))
+        store(G - 1, vector_copy, slice(N // 2, N))

from contextlib import ExitStack

import concourse.mybir as mybir

G, D, K, M, N = 4, 128, 1024, 128, 512
FLOPS = 2 * G * N * (D * K + K * M)

F32 = mybir.dt.float32
BF16 = mybir.dt.bfloat16
U32 = mybir.dt.uint32
U8 = mybir.dt.uint8
FP8X4 = mybir.dt.float8_e4m3fn_x4
ALU = mybir.AluOpType
ACT = mybir.ActivationFunctionType

P = 128
PACK = 4
ROWS = D // PACK
K_PASS = P * PACK
PASSES = K // K_PASS
UNITS = G * PASSES
RUN = 2
QUAD = 32
TINY = 2.0 ** -100
SCALAR_COLS = 160
SCALAR_COLS_LAST = 256
SCALAR_COLS_6 = 256
AHEAD = 2
G1_SCALAR = True


def tile_rows_gmlp_relu2_bias_kernel(tc, x, w1, hs, w2, b, out):
    nc = tc.nc

    def runs_of_rows(rows):
        return rows.rearrange("p j (c i) -> p c j i", i=RUN)

    def runs_of_words(words):
        return words.rearrange("p (c i) j -> p c j i", i=RUN)

    def quantize(codes, scales, words):
        nc.vector.quantize_mx(out=codes.bitcast(FP8X4), scales=scales, in_=words.rearrange("p c j -> p (c j)"))

    with ExitStack() as ctx:
        sb = ctx.enter_context(tc.tile_pool(name="sb", bufs=1))
        ps = ctx.enter_context(tc.psum_pool(name="ps", bufs=1))
        ctx.enter_context(tc.manual_schedule())

        def sbuf(name, shape, dtype):
            return sb.tile(shape, dtype, name=name, align_bytes=64)

        def vector_copy(o, i):
            nc.vector.tensor_copy(out=o, in_=i)

        def scalar_copy(o, i):
            nc.scalar.copy(out=o, in_=i)

        vec_raw = sbuf("vec_raw", [P, P], F32)
        nc.vector.memset(vec_raw[:], 0.0)

        x_raw = sbuf("x_raw", [P, PACK, N], F32)
        w1_rows = w1.rearrange("g (p j) k -> (g p) j k", j=PACK)
        w1_raw = [sbuf("w1_raw%d" % q, [P, PACK, K_PASS], F32) for q in range(PASSES)]
        w2_raw = [sbuf("w2_raw%d" % g, [P, PASSES, PACK, M], F32) for g in range(G)]

        def load_w1(q):
            nc.sync.dma_start(out=w1_raw[q][:], in_=w1_rows[:, :, q * K_PASS : (q + 1) * K_PASS])

        def load_w2(g):
            nc.sync.dma_start(
                out=w2_raw[g][:].rearrange("p q j m -> p q (j m)"),
                in_=w2[g].rearrange("(q p j) m -> p q (j m)", q=PASSES, j=PACK),
            )

        nc.sync.dma_start(
            out=x_raw[:].rearrange("p j n -> p (j n)"), in_=x.rearrange("g (p j) n -> (g p) (j n)", j=PACK)
        )
        for place, vec in enumerate((b, hs)):
            nc.sync.dma_start(
                out=vec_raw[place:P:PACK, :],
                in_=vec.rearrange("g (q d w) o -> d (g q) (w o)", q=PASSES, d=P // QUAD),
            )
        load_w1(0)
        for g in range(G - 1):
            load_w2(g)
        load_w1(1)
        load_w2(G - 1)

        x_bf = sbuf("x_bf", [P, N, PACK], BF16)
        x_codes = sbuf("x_codes", [P, N], U32)
        x_scales = sbuf("x_scales", [P, N], U8)

        vec_dealt = sbuf("vec_dealt", [P, PACK, QUAD], F32)
        vec_t = sbuf("vec_t", [P, PACK, QUAD], F32)
        nc.vector.tensor_copy(out=vec_dealt[:], in_=vec_raw[:].rearrange("p (a r) -> p r a", r=PACK))
        vector_copy(runs_of_words(x_bf[:]), runs_of_rows(x_raw[:]))
        nc.vector.transpose(out=vec_t[:].rearrange("p r c -> p (r c)"), in_=vec_dealt[:].rearrange("p r a -> p (r a)"))
        vec_cols = vec_t[:].rearrange("p r (u w) -> p u r w", w=PACK)
        b_tab = vec_cols[:, :, :, 0]
        hs_tab = vec_cols[:, :, :, 1]
        mag = sbuf("mag", [P, UNITS, PACK], F32)
        root0 = sbuf("root0", [P, UNITS, PACK], F32)
        sgn = sbuf("sgn", [P, UNITS, PACK], F32)
        inv = sbuf("inv", [P, UNITS, PACK], F32)
        half_q = sbuf("half_q", [P, UNITS, PACK], F32)
        root = sbuf("root", [P, UNITS, PACK], F32)
        root_b = sbuf("root_b", [P, UNITS, PACK], F32)
        nc.vector.scalar_tensor_tensor(out=mag[:], in0=hs_tab, scalar=-1.0, in1=hs_tab, op0=ALU.mult, op1=ALU.max)
        nc.scalar.activation(out=root0[:], in_=mag[:], func=ACT.Sqrt, bias=TINY)
        nc.scalar.activation(out=sgn[:], in_=hs_tab, func=ACT.Sign)

        halves = [(q, h) for q in range(PASSES) for h in range(PACK // RUN)]
        w1_bf = {k: sbuf("w1_bf%d%d" % k, [P, RUN * P, PACK], BF16) for k in halves}
        w1_codes = {k: sbuf("w1_codes%d%d" % k, [P, RUN * P], U32) for k in halves}
        w1_scales = {k: sbuf("w1_scales%d%d" % k, [P, RUN * P], U8) for k in halves}

        def round_w1(q, h, copy):
            copy(
                w1_bf[q, h][:].rearrange("p (r m) j -> p m j r", r=RUN),
                w1_raw[q][:].rearrange("p j (m r) -> p m j r", r=PACK)[:, :, :, h * RUN : (h + 1) * RUN],
            )

        def quantize_w1(q, h):
            quantize(w1_codes[q, h][:], w1_scales[q, h][:], w1_bf[q, h][:])

        quantize(x_codes[:], x_scales[:], x_bf[:])
        round_w1(0, 0, vector_copy)
        round_w1(0, 1, scalar_copy)
        nc.vector.reciprocal(out=inv[:], in_=root0[:])
        quantize_w1(0, 0)
        nc.vector.scalar_tensor_tensor(out=half_q[:], in0=mag[:], scalar=0.5, in1=inv[:], op0=ALU.mult, op1=ALU.mult)
        quantize_w1(0, 1)
        nc.vector.scalar_tensor_tensor(out=root[:], in0=root0[:], scalar=0.5, in1=half_q[:], op0=ALU.mult, op1=ALU.add)
        nc.vector.tensor_tensor(out=root_b[:], in0=root[:], in1=b_tab, op=ALU.mult)

        w2_bf = [sbuf("w2_bf%d" % c, [P, M, PACK], BF16) for c in range(UNITS)]
        w2_codes = [sbuf("w2_codes%d" % c, [P, M], U32) for c in range(UNITS)]
        w2_scales = [sbuf("w2_scales%d" % c, [P, M], U8) for c in range(UNITS)]

        def round_w2(g, q):
            c = g * PASSES + q
            nc.vector.tensor_tensor(
                out=runs_of_words(w2_bf[c][:]),
                in0=runs_of_rows(w2_raw[g][:, q, :, :]),
                in1=sgn[:, c, :].unsqueeze(1).unsqueeze(3).to_broadcast([P, M // RUN, PACK, RUN]),
                op=ALU.mult,
            )

        def quantize_w2(g, q):
            c = g * PASSES + q
            quantize(w2_codes[c][:], w2_scales[c][:], w2_bf[c][:])

        early = [(g, q) for g in range(G - 1) for q in range(PASSES)]
        round_w2(*early[0])
        for i in range(1, len(early)):
            round_w2(*early[i])
            quantize_w2(*early[i - 1])

        n_banks = [2, 1, 1, 2]
        banks = [[ps.tile([P, N], F32, name="z%d_%d" % (g, i)) for i in range(n_banks[g])] for g in range(G)]
        acc = [ps.tile([P, N], F32, name="acc%d" % i) for i in range(2)]
        act = [sbuf("act%d" % u, [P, PACK, N], F32) for u in range(UNITS)]
        h_bf = [sbuf("h_bf%d" % u, [P, N, PACK], BF16) for u in range(UNITS)]
        h_codes = [sbuf("h_codes%d" % u, [P, N], U32) for u in range(UNITS)]
        h_scales = [sbuf("h_scales%d" % u, [P, N], U8) for u in range(UNITS)]
        res = [sbuf("res%d" % g, [P, N], F32) for g in range(G)]

        steps = sorted(((u, r) for u in range(UNITS) for r in range(PACK)), key=lambda s: 4 * s[0] + 3 * s[1])

        steps[1:3] = [steps[2], steps[1]]

        def bank_of(u, r):
            g, q = u % G, u // G
            return banks[g][(q * PACK + r) % n_banks[g]]

        def first_layer(u, r):
            g, q = u % G, u // G
            rows = slice(g * ROWS, (g + 1) * ROWS)
            cols = slice(r % RUN * P, (r % RUN + 1) * P)
            nc.tensor.matmul_mx(
                out=bank_of(u, r)[:],
                lhsT=w1_codes[q, r // RUN][rows, cols].bitcast(FP8X4),
                lhsT_scale=w1_scales[q, r // RUN][rows, cols],
                rhs=x_codes[rows, :].bitcast(FP8X4),
                rhs_scale=x_scales[rows, :],
                start=True,
                stop=True,
            )

        def relu(u, r):
            g, q = u % G, u // G
            c = g * PASSES + q
            nc.scalar.activation(
                out=act[u][:, r, :],
                in_=bank_of(u, r)[:],
                func=ACT.Relu,
                scale=root[:, c, r : r + 1],
                bias=root_b[:, c, r : r + 1],
            )

        def scalar_cols(u):
            return SCALAR_COLS_LAST if u == UNITS - 1 else (SCALAR_COLS_6 if u == UNITS - 2 else SCALAR_COLS)

        def square_vector(u):
            rows = runs_of_rows(act[u][:, :, scalar_cols(u) :])
            nc.vector.tensor_tensor(out=runs_of_words(h_bf[u][:, scalar_cols(u) :, :]), in0=rows, in1=rows, op=ALU.mult)

        def square_scalar(u):
            nc.scalar.activation(
                out=runs_of_words(h_bf[u][:, : scalar_cols(u), :]),
                in_=runs_of_rows(act[u][:, :, : scalar_cols(u)]),
                func=ACT.Square,
            )

        def second_layer(g, q):
            u, c = q * G + g, g * PASSES + q
            nc.tensor.matmul_mx(
                out=acc[g % 2][:],
                lhsT=w2_codes[c][:].bitcast(FP8X4),
                lhsT_scale=w2_scales[c][:],
                rhs=h_codes[u][:].bitcast(FP8X4),
                rhs_scale=h_scales[u][:],
                start=(q == 0),
                stop=(q == PASSES - 1),
            )

        def store(g, engine_copy, cols=slice(0, N)):
            engine_copy(res[g][:, cols], acc[g % 2][:, cols])
            nc.sync.dma_start(out=out[g][:, cols], in_=res[g][:, cols])

        def quantize_h(u, cols):
            quantize(h_codes[u][:, cols], h_scales[u][:, cols], h_bf[u][:, cols, :])

        def finish(u):
            square_scalar(u)
            if u == 0:
                quantize_w2(*early[-1])
            if u < 2:
                round_w1(1, u, vector_copy)
            elif u < 4:
                round_w2(G - 1, u - 2)
            if u == G + 1:
                store(0, vector_copy)
            if u == G + 2 and not G1_SCALAR:
                store(1, vector_copy)
            quantize_h(u, slice(0, N))
            if u < 2:
                quantize_w1(1, u)
            elif u < 4:
                quantize_w2(G - 1, u - 2)

        for s in steps[:AHEAD]:
            first_layer(*s)
        pending = None
        for i, (u, r) in enumerate(steps):
            relu(u, r)
            if i + AHEAD < len(steps):
                first_layer(*steps[i + AHEAD])
            if pending is not None:
                finish(pending)
                pending = None
            if r == PACK - 1:
                square_vector(u)
                pending = u
                if u - 1 in (0, 1, G, G + 1):
                    second_layer((u - 1) % G, (u - 1) // G)
                if u == G + 2:
                    second_layer(2, 0)
        last = UNITS - 1
        second_layer(2, 1)
        if G1_SCALAR:
            store(1, scalar_copy)
        second_layer(3, 0)
        square_scalar(last)
        quantize_h(last, slice(N // 2, N))
        quantize_h(last, slice(0, N // 2))
        second_layer(G - 1, 1)
        store(G - 2, scalar_copy)
        store(G - 1, vector_copy, slice(0, N // 2))
        store(G - 1, vector_copy, slice(N // 2, N))
